import numpy as np
import ml_dtypes


def mxq(x, axis, fmt="e4m3"):
    dtype, down = {"e4m3": (ml_dtypes.float8_e4m3fn, 7), "e5m2": (ml_dtypes.float8_e5m2, 14)}[fmt]
    v = np.moveaxis(np.asarray(x, np.float32).astype(ml_dtypes.bfloat16).astype(np.float64), axis, -1)
    blocks = v.reshape(v.shape[:-1] + (-1, 32))
    amax = np.abs(blocks).max(-1, keepdims=True)
    byte = np.maximum(np.where(amax > 0, np.frexp(amax)[1] - 1 + 127, 0) - down, 1)
    scale = np.exp2(byte - 127.0)
    codes = (blocks / scale).astype(np.float32).astype(dtype).astype(np.float64)
    return np.moveaxis((codes * scale).reshape(v.shape), -1, axis)


WIDE = False


def mx_kscale(k):
    if not WIDE:
        return np.ones(k)
    levels = np.array([10, -10, 5, -5, 0])
    if k % 512:
        return np.exp2(np.random.permutation(np.resize(levels, k // 32))).repeat(32)
    a = np.empty((k // 512, 16))
    for p in range(k // 512):
        a[p, :8] = np.random.permutation(np.resize(levels, 8))
        for g in range(8):
            far = levels[np.abs(levels - a[p, g]) >= 10]
            a[p, g + 8] = far[np.random.randint(len(far))]
    return np.exp2(a.ravel()).repeat(32)


def f64(x):
    return np.asarray(x).astype(np.float64)


def striped(idx):
    return np.tile(idx.reshape(-1, 16).T, (8, 1)).astype(np.uint16)


def unstriped(offs):
    return offs[:16].T.reshape(-1).astype(np.int64)


def striped8(idx):
    return np.concatenate([x.reshape(-1, 16).T for x in idx]).astype(np.uint16)


def runs(offs, k):
    lists = np.stack([offs[16 * r : 16 * r + 16].T.reshape(-1) for r in range(8)]).astype(np.int64)
    return lists[np.arange(k) % 512 // 64]


def pack_weight(w):
    k, n = w.shape
    w = f64(np.asarray(w, np.float32).astype(ml_dtypes.bfloat16)).reshape(k // 32, 32, n)
    amax = np.abs(w).max(1)
    byte = np.clip(np.where(amax > 0, np.frexp(amax)[1] - 1 + 127 - 7, 1), 1, 254)
    scaled = (w * np.exp2(127.0 - byte)[:, None, :]).reshape(k, n).astype(np.float32)
    words = np.ascontiguousarray(scaled.reshape(k // 512, 128, 4, n).transpose(0, 1, 3, 2)).astype(ml_dtypes.float8_e4m3fn).view(np.uint8)
    return words, np.ascontiguousarray(byte.astype(np.uint8).reshape(k // 512, 16, n))


def unpack_weight(words, scales):
    g, p, n, _ = words.shape
    vals = np.ascontiguousarray(words).view(ml_dtypes.float8_e4m3fn).astype(np.float64) * np.repeat(np.exp2(scales.astype(np.float64) - 127.0), 8, axis=1)[..., None]
    return vals.transpose(0, 1, 3, 2).reshape(g * 512, n)


E2M1 = np.array([0.0, 0.5, 1.0, 1.5, 2.0, 3.0, 4.0, 6.0, -0.0, -0.5, -1.0, -1.5, -2.0, -3.0, -4.0, -6.0])


def pack_fp4(w):
    k, n = w.shape
    w = f64(np.asarray(w, np.float32).astype(ml_dtypes.bfloat16)).reshape(k // 32, 32, n)
    amax = np.abs(w).max(1)
    mant, ex = np.frexp(amax / 6.0)
    byte = np.clip(np.where(amax > 0, np.where(mant > 0.5, ex, ex - 1) + 127, 1), 1, 254)
    scaled = (w * np.exp2(127.0 - byte)[:, None, :]).reshape(k, n).astype(np.float32)
    c = np.ascontiguousarray(scaled.reshape(k // 512, 128, 4, n).transpose(0, 1, 3, 2)).astype(ml_dtypes.float4_e2m1fn).view(np.uint8) & 0xF
    words = (c[..., 0::2] | (c[..., 1::2] << 4)).reshape(k // 512, 128, 2 * n)
    return np.ascontiguousarray(words), np.ascontiguousarray(byte.astype(np.uint8).reshape(k // 512, 16, n))


def unpack_fp4(words, scales):
    g, _, n = scales.shape
    words = np.ascontiguousarray(words).reshape(g, 128, n, 2)
    nib = np.empty((g, 128, n, 4), np.uint8)
    nib[..., 0::2] = words & 0xF
    nib[..., 1::2] = words >> 4
    vals = E2M1[nib] * np.repeat(np.exp2(scales.astype(np.float64) - 127.0), 8, axis=1)[..., None]
    return vals.transpose(0, 1, 3, 2).reshape(g * 512, n)


def sigmoid(v):
    return 1.0 / (1.0 + np.exp(-np.maximum(v, -700.0)))

def planes(y):
    n, m = y.shape
    v = y.astype(np.float32).astype(ml_dtypes.bfloat16).astype(np.float64).reshape(n // 32, 32, m)
    top = np.abs(v).max(1)
    byte = np.clip(np.where(top > 0, np.frexp(top)[1] - 1 + 127 - 7, 1), 1, 254)
    codes = (v * np.exp2(127.0 - byte)[:, None, :]).reshape(n, m).astype(np.float32).astype(ml_dtypes.float8_e4m3fn).view(np.uint8)
    words = codes.reshape(n // 512, 128, 4, m).transpose(0, 1, 3, 2)
    return np.ascontiguousarray(words), np.ascontiguousarray(byte.astype(np.uint8).reshape(n // 512, 16, m))


K, T, S, V, N, H = 512, 2048, 512, 256, 512, 512


def setup_inputs():
    n = np.random.standard_normal
    s = mx_kscale(K)[:, None]
    u = mx_kscale(H)
    packed_xT = pack_weight(n((K, T)) * s)
    packed_w1 = pack_fp4(n((K, H)) / np.sqrt(K) / s)
    packed_w2 = pack_fp4(n((H, N)) / np.sqrt(H) / u[:, None])
    perm = np.stack([np.random.permutation(S) for _ in range(8)])
    return {
        "x_words": packed_xT[0],
        "x_scales": packed_xT[1],
        "w1_words": packed_w1[0],
        "w1_scales": packed_w1[1],
        "gn": (np.random.uniform(0.5, 1.5, (H, 1)) * u[:, None]).astype(np.float32),
        "w2_words": packed_w2[0],
        "w2_scales": packed_w2[1],
        "offs": striped(np.random.permutation(T)[:S]),
        "la": striped8(perm[:, :V]),
        "lb": striped8(perm[:, V:]),
    }


def reference(x_words, x_scales, w1_words, w1_scales, gn, w2_words, w2_scales, offs, la, lb):
    xq = unpack_weight(x_words, x_scales)[:, unstriped(offs)]
    y = unpack_fp4(w1_words, w1_scales).T @ xq
    b = y[np.arange(H)[:, None], runs(lb, H)]
    a = y[np.arange(H)[:, None], runs(la, H)]
    mn = b + a * sigmoid(a)
    h = y.copy()
    h[np.arange(H)[:, None], runs(lb, H)] = mn
    z = f64(gn) * h
    o = unpack_fp4(w2_words, w2_scales).T @ mxq(z, 0, "e4m3")
    out_0 = o
    return (out_0,) + planes(out_0)

@@ -1,0 +1,183 @@
+from contextlib import ExitStack
+
+import concourse.mybir as mybir
+
+K, T, S, V, H, N = 512, 2048, 512, 256, 512, 512
+FLOPS = 2 * K * H * S + 2 * H * N * S
+
+F32 = mybir.dt.float32
+BF16 = mybir.dt.bfloat16
+I32 = mybir.dt.int32
+U32 = mybir.dt.uint32
+U16 = mybir.dt.uint16
+U8 = mybir.dt.uint8
+FP8X4 = mybir.dt.float8_e4m3fn_x4
+FP4X4 = mybir.dt.float4_e2m1fn_x4
+ACT = mybir.ActivationFunctionType
+ALU = mybir.AluOpType
+
+P = 128
+PACK = 4
+HALF = S // 2
+CHUNK = 128
+CHUNKS = S // CHUNK
+ORDER = (0, 2, 3, 1)
+
+
+def load_scale_rows(queues, tile, scales):
+    for q in range(4):
+        queues[q].dma_start(
+            out=tile[32 * q : 32 * q + 4, :].bitcast(I32),
+            in_=scales[0, 4 * q : 4 * q + 4, :].bitcast(I32),
+        )
+
+
+def deal_words(nc, dealt, words, ts):
+    nc.vector.tensor_copy(
+        out=dealt[:].rearrange("p t (m b) -> p t m b", b=2),
+        in_=words[:].rearrange("p (m t b) -> p t m b", t=PACK, b=2)[:, ts],
+    )
+
+
+def deal_scales(nc, dealt, scales):
+    nc.vector.tensor_copy(out=dealt[:], in_=scales[:].rearrange("p (m t) -> p t m", t=PACK))
+
+
+def tile_picked_revcoup_none_po_kernel(
+    tc, x_words, x_scales, w1_words, w1_scales, gn, w2_words, w2_scales, offs, la, lb, out_0, out_1, out_2
+):
+    nc = tc.nc
+    with ExitStack() as ctx:
+        keep = ctx.enter_context(tc.tile_pool(name="keep", bufs=1))
+        psum = ctx.enter_context(tc.psum_pool(name="psum", bufs=8))
+
+        offs_t = keep.tile([P, S // 16], U16, name="offs_t")
+        la_t = keep.tile([P, V // 16], U16, name="la_t")
+        lb_t = keep.tile([P, V // 16], U16, name="lb_t")
+        xw = keep.tile([P, T], U32, name="xw", align_bytes=64)
+        xs = keep.tile([P, T], U8, name="xs", align_bytes=64)
+        w1w = keep.tile([P, 2 * H], U8, name="w1w", align_bytes=64)
+        w1s = keep.tile([P, H], U8, name="w1s", align_bytes=64)
+        w2s = keep.tile([P, N], U8, name="w2s", align_bytes=64)
+        gn_t = keep.tile([P, PACK], F32, name="gn_t")
+        warm = keep.tile([P, 2], F32, name="warm")
+
+        nc.vector.memset(xs[:].bitcast(I32), 0)
+        nc.vector.memset(w1s[:].bitcast(I32), 0)
+        nc.vector.memset(w2s[:].bitcast(I32), 0)
+        nc.vector.memset(warm[:, 0:1], 0.0)
+
+        nc.sync.dma_start(offs_t[:], offs)
+        nc.sync.dma_start(la_t[:], la)
+        nc.sync.dma_start(lb_t[:], lb)
+        nc.sync.dma_start(out=xw[:].bitcast(I32), in_=x_words[0].rearrange("p c r -> p (c r)").bitcast(I32))
+        nc.gpsimd.dma_start(out=w1w[:].bitcast(I32), in_=w1_words[0].bitcast(I32))
+        load_scale_rows([nc.scalar] * 4, xs, x_scales)
+        load_scale_rows([nc.sync] * 3 + [nc.gpsimd], w1s, w1_scales)
+        nc.scalar.activation(out=warm[:, 1:2], in_=warm[:, 0:1], func=ACT.Silu)
+        load_scale_rows([nc.sync] * 4, w2s, w2_scales)
+        nc.gpsimd.dma_start(out=gn_t[:], in_=gn.rearrange("(p t) o -> p (t o)", t=PACK))
+
+        first, last = ORDER[0], ORDER[-1]
+        xsg = keep.tile([P, S], U8, name="xsg", align_bytes=64)
+        nc.vector.tensor_copy(xsg[:], xs[:].indirect(offs_t[:]))
+        w2w = keep.tile([P, 2 * N], U8, name="w2w", tag="xs", align_bytes=64)
+        nc.sync.dma_start(out=w2w[:].bitcast(I32), in_=w2_words[0].bitcast(I32))
+
+        w1d_first = keep.tile([P, 1, 2 * P], U8, name="w1d_first", align_bytes=64)
+        deal_words(nc, w1d_first, w1w, slice(0, 1))
+        w1sd = keep.tile([P, PACK, P], U8, name="w1sd", align_bytes=64)
+        deal_scales(nc, w1sd, w1s)
+        xg = keep.tile([P, S], U32, name="xg", tag="w1s", align_bytes=64)
+        for u in range(2):
+            nc.vector.tensor_copy(
+                xg[:, u * HALF : (u + 1) * HALF],
+                xw[:].indirect(offs_t[:, u * HALF // 16 : (u + 1) * HALF // 16]),
+            )
+        w1d_rest = keep.tile([P, PACK - 1, 2 * P], U8, name="w1d_rest", tag="xw", align_bytes=64)
+        deal_words(nc, w1d_rest, w1w, slice(1, PACK))
+        w2sd = keep.tile([P, PACK, P], U8, name="w2sd", tag="w1w", align_bytes=64)
+        deal_scales(nc, w2sd, w2s)
+
+        def first_product(acc, t, cols):
+            nc.tensor.matmul_mx(
+                out=acc,
+                lhsT=(w1d_first[:, 0, :] if t == 0 else w1d_rest[:, t - 1, :]).bitcast(FP4X4),
+                lhsT_scale=w1sd[:, t, :],
+                rhs=xg[:, cols].bitcast(FP8X4),
+                rhs_scale=xsg[:, cols],
+                start=True,
+                stop=True,
+            )
+
+        z = [keep.tile([P, CHUNK, PACK], BF16, name=f"z{c}", align_bytes=64) for c in range(CHUNKS)]
+        w2d = {}
+        for t in ORDER:
+            h = keep.tile([P, S], F32, name=f"h{t}", tag=f"h{first if t == last else t}")
+            act = keep.tile([P, S], F32, name=f"act{t}", align_bytes=64)
+            for cols in [slice(0, HALF), slice(HALF, S)] if t == first else [slice(0, S)]:
+                y = psum.tile([P, S], F32, name=f"y{t}", tag="bank")
+                width = cols.stop - cols.start
+                first_product(y[:, 0:width], t, cols)
+                nc.scalar.activation(out=act[:, cols], in_=y[:, 0:width], func=ACT.Silu)
+                nc.scalar.copy(out=h[:, cols], in_=y[:, 0:width])
+            ga = keep.tile([P, V], F32, name=f"ga{t}")
+            gb = keep.tile([P, V], F32, name=f"gb{t}")
+            nc.vector.tensor_copy(ga[:], act[:].indirect(la_t[:]))
+            nc.vector.tensor_copy(gb[:], h[:].indirect(lb_t[:]))
+            w2d[t] = keep.tile([P, 1, 2 * P], U8, name=f"w2d{t}", tag=f"act{t}", align_bytes=64)
+            deal_words(nc, w2d[t], w2w, slice(t, t + 1))
+            nc.vector.tensor_tensor(h[:].indirect(lb_t[:]), gb[:], ga[:], ALU.add)
+            for c in range(CHUNKS):
+                cols = slice(c * CHUNK, (c + 1) * CHUNK)
+                if t == last:
+                    nc.vector.tensor_scalar(
+                        out=z[c][:, :, t], in0=h[:, cols], scalar1=gn_t[:, t : t + 1], scalar2=None, op0=ALU.mult
+                    )
+                else:
+                    nc.scalar.activation(out=z[c][:, :, t], in_=h[:, cols], func=ACT.Copy, scale=gn_t[:, t : t + 1])
+
+        oq = keep.tile([P, S], U32, name="oq", align_bytes=64)
+        osc = keep.tile([P, S], U8, name="osc", align_bytes=64)
+        out_rows = out_0.rearrange("(p t) c -> p t c", t=PACK)
+        out_words = out_1[0].rearrange("p c r -> p (c r)").bitcast(I32)
+        accs = []
+        for c in range(CHUNKS):
+            zq = keep.tile([P, CHUNK], U32, name=f"zq{c}", align_bytes=64)
+            zsc = keep.tile([P, CHUNK], U8, name=f"zsc{c}", align_bytes=64)
+            nc.vector.quantize_mx(out=zq[:].bitcast(FP8X4), scales=zsc[:], in_=z[c][:].rearrange("p c t -> p (c t)"))
+            acc = psum.tile([P, PACK, CHUNK], F32, name=f"o{c}", tag="bank")
+            for t in range(PACK):
+                nc.tensor.matmul_mx(
+                    out=acc[:, t, :],
+                    lhsT=w2d[t][:, 0, :].bitcast(FP4X4),
+                    lhsT_scale=w2sd[:, t, :],
+                    rhs=zq[:].bitcast(FP8X4),
+                    rhs_scale=zsc[:],
+                    start=True,
+                    stop=True,
+                )
+            accs.append(acc)
+        for c in range(CHUNKS):
+            cols = slice(c * CHUNK, (c + 1) * CHUNK)
+            o32 = keep.tile([P, PACK, CHUNK], F32, name=f"o32{c}")
+            ob = keep.tile([P, CHUNK, PACK], BF16, name=f"ob{c}", align_bytes=64)
+            if c == CHUNKS - 1:
+                nc.vector.tensor_copy(out=ob[:], in_=accs[c][:].rearrange("p t c -> p c t"))
+            nc.scalar.copy(out=o32[:], in_=accs[c][:])
+            nc.sync.dma_start(out=out_rows[:, :, cols], in_=o32[:])
+            if c < CHUNKS - 1:
+                nc.vector.tensor_copy(
+                    out=ob[:].rearrange("p (c i) t -> p c t i", i=4),
+                    in_=o32[:].rearrange("p t (c i) -> p c t i", i=4),
+                )
+            nc.vector.quantize_mx(out=oq[:, cols].bitcast(FP8X4), scales=osc[:, cols], in_=ob[:].rearrange("p c t -> p (c t)"))
+            if c >= CHUNKS - 2:
+                done = slice(0, (c + 1) * CHUNK) if c == CHUNKS - 2 else cols
+                nc.sync.dma_start(out=out_words[:, done], in_=oq[:, done].bitcast(I32))
+        for q in range(4):
+            queue = nc.scalar if q % 2 == 0 else nc.sync
+            queue.dma_start(
+                out=out_2[0, 4 * q : 4 * q + 4, :].bitcast(I32),
+                in_=osc[32 * q : 32 * q + 4, :].bitcast(I32),
+            )

@@ -21,7 +21,6 @@ PACK = 4
 HALF = S // 2
 CHUNK = 128
 CHUNKS = S // CHUNK
-ORDER = (0, 2, 3, 1)
 
 
 def load_scale_rows(queues, tile, scales):
@@ -32,10 +31,10 @@ def load_scale_rows(queues, tile, scales):
         )
 
 
-def deal_words(nc, dealt, words, ts):
+def deal_words(nc, dealt, words):
     nc.vector.tensor_copy(
         out=dealt[:].rearrange("p t (m b) -> p t m b", b=2),
-        in_=words[:].rearrange("p (m t b) -> p t m b", t=PACK, b=2)[:, ts],
+        in_=words[:].rearrange("p (m t b) -> p t m b", t=PACK, b=2),
     )
 
 
@@ -58,6 +57,7 @@ def tile_picked_revcoup_none_po_kernel(
         xs = keep.tile([P, T], U8, name="xs", align_bytes=64)
         w1w = keep.tile([P, 2 * H], U8, name="w1w", align_bytes=64)
         w1s = keep.tile([P, H], U8, name="w1s", align_bytes=64)
+        w2w = keep.tile([P, 2 * N], U8, name="w2w", align_bytes=64)
         w2s = keep.tile([P, N], U8, name="w2s", align_bytes=64)
         gn_t = keep.tile([P, PACK], F32, name="gn_t")
         warm = keep.tile([P, 2], F32, name="warm")
@@ -68,25 +68,24 @@ def tile_picked_revcoup_none_po_kernel(
         nc.vector.memset(warm[:, 0:1], 0.0)
 
         nc.sync.dma_start(offs_t[:], offs)
+        nc.scalar.dma_start(out=w1w[:].bitcast(I32), in_=w1_words[0].bitcast(I32))
         nc.sync.dma_start(la_t[:], la)
-        nc.sync.dma_start(lb_t[:], lb)
+        load_scale_rows([nc.sync, nc.scalar] * 2, xs, x_scales)
         nc.sync.dma_start(out=xw[:].bitcast(I32), in_=x_words[0].rearrange("p c r -> p (c r)").bitcast(I32))
-        nc.gpsimd.dma_start(out=w1w[:].bitcast(I32), in_=w1_words[0].bitcast(I32))
-        load_scale_rows([nc.scalar] * 4, xs, x_scales)
-        load_scale_rows([nc.sync] * 3 + [nc.gpsimd], w1s, w1_scales)
         nc.scalar.activation(out=warm[:, 1:2], in_=warm[:, 0:1], func=ACT.Silu)
-        load_scale_rows([nc.sync] * 4, w2s, w2_scales)
-        nc.gpsimd.dma_start(out=gn_t[:], in_=gn.rearrange("(p t) o -> p (t o)", t=PACK))
-
-        first, last = ORDER[0], ORDER[-1]
-        xsg = keep.tile([P, S], U8, name="xsg", align_bytes=64)
-        nc.vector.tensor_copy(xsg[:], xs[:].indirect(offs_t[:]))
-        w2w = keep.tile([P, 2 * N], U8, name="w2w", tag="xs", align_bytes=64)
+        load_scale_rows([nc.scalar] * 4, w1s, w1_scales)
+        nc.sync.dma_start(lb_t[:], lb)
         nc.sync.dma_start(out=w2w[:].bitcast(I32), in_=w2_words[0].bitcast(I32))
+        load_scale_rows([nc.sync] * 4, w2s, w2_scales)
+        nc.sync.dma_start(out=gn_t[:], in_=gn.rearrange("(p t) o -> p (t o)", t=PACK))
 
-        w1d_first = keep.tile([P, 1, 2 * P], U8, name="w1d_first", align_bytes=64)
-        deal_words(nc, w1d_first, w1w, slice(0, 1))
+        xsg = keep.tile([P, S], U8, name="xsg", align_bytes=64)
+        w1d = keep.tile([P, PACK, 2 * P], U8, name="w1d", align_bytes=64)
         w1sd = keep.tile([P, PACK, P], U8, name="w1sd", align_bytes=64)
+        w2d = keep.tile([P, PACK, 2 * P], U8, name="w2d", align_bytes=64)
+        w2sd = keep.tile([P, PACK, P], U8, name="w2sd", align_bytes=64)
+        deal_words(nc, w1d, w1w)
+        nc.vector.tensor_copy(xsg[:], xs[:].indirect(offs_t[:]))
         deal_scales(nc, w1sd, w1s)
         xg = keep.tile([P, S], U32, name="xg", tag="w1s", align_bytes=64)
         for u in range(2):
@@ -94,89 +93,87 @@ def tile_picked_revcoup_none_po_kernel(
                 xg[:, u * HALF : (u + 1) * HALF],
                 xw[:].indirect(offs_t[:, u * HALF // 16 : (u + 1) * HALF // 16]),
             )
-        w1d_rest = keep.tile([P, PACK - 1, 2 * P], U8, name="w1d_rest", tag="xw", align_bytes=64)
-        deal_words(nc, w1d_rest, w1w, slice(1, PACK))
-        w2sd = keep.tile([P, PACK, P], U8, name="w2sd", tag="w1w", align_bytes=64)
+        deal_words(nc, w2d, w2w)
         deal_scales(nc, w2sd, w2s)
 
-        def first_product(acc, t, cols):
-            nc.tensor.matmul_mx(
-                out=acc,
-                lhsT=(w1d_first[:, 0, :] if t == 0 else w1d_rest[:, t - 1, :]).bitcast(FP4X4),
-                lhsT_scale=w1sd[:, t, :],
-                rhs=xg[:, cols].bitcast(FP8X4),
-                rhs_scale=xsg[:, cols],
-                start=True,
-                stop=True,
-            )
-
         z = [keep.tile([P, CHUNK, PACK], BF16, name=f"z{c}", align_bytes=64) for c in range(CHUNKS)]
-        w2d = {}
-        for t in ORDER:
-            h = keep.tile([P, S], F32, name=f"h{t}", tag=f"h{first if t == last else t}")
-            act = keep.tile([P, S], F32, name=f"act{t}", align_bytes=64)
-            for cols in [slice(0, HALF), slice(HALF, S)] if t == first else [slice(0, S)]:
+        for t in range(PACK):
+            h = keep.tile([P, S], F32, name=f"h{t}")
+            ys = keep.tile([P, S], F32, name=f"ys{t}")
+            act = keep.tile([P, S], F32, name=f"act{t}")
+            for cols in [slice(0, HALF), slice(HALF, S)] if t == 0 else [slice(0, S)]:
                 y = psum.tile([P, S], F32, name=f"y{t}", tag="bank")
                 width = cols.stop - cols.start
-                first_product(y[:, 0:width], t, cols)
+                nc.tensor.matmul_mx(
+                    out=y[:, 0:width],
+                    lhsT=w1d[:, t, :].bitcast(FP4X4),
+                    lhsT_scale=w1sd[:, t, :],
+                    rhs=xg[:, cols].bitcast(FP8X4),
+                    rhs_scale=xsg[:, cols],
+                    start=True,
+                    stop=True,
+                )
                 nc.scalar.activation(out=act[:, cols], in_=y[:, 0:width], func=ACT.Silu)
-                nc.scalar.copy(out=h[:, cols], in_=y[:, 0:width])
+                nc.scalar.copy(out=ys[:, cols], in_=y[:, 0:width])
+            nc.sync.dma_start(out=h[:], in_=ys[:])
             ga = keep.tile([P, V], F32, name=f"ga{t}")
             gb = keep.tile([P, V], F32, name=f"gb{t}")
             nc.vector.tensor_copy(ga[:], act[:].indirect(la_t[:]))
-            nc.vector.tensor_copy(gb[:], h[:].indirect(lb_t[:]))
-            w2d[t] = keep.tile([P, 1, 2 * P], U8, name=f"w2d{t}", tag=f"act{t}", align_bytes=64)
-            deal_words(nc, w2d[t], w2w, slice(t, t + 1))
+            nc.vector.tensor_copy(gb[:], ys[:].indirect(lb_t[:]))
             nc.vector.tensor_tensor(h[:].indirect(lb_t[:]), gb[:], ga[:], ALU.add)
             for c in range(CHUNKS):
                 cols = slice(c * CHUNK, (c + 1) * CHUNK)
-                if t == last:
-                    nc.vector.tensor_scalar(
-                        out=z[c][:, :, t], in0=h[:, cols], scalar1=gn_t[:, t : t + 1], scalar2=None, op0=ALU.mult
-                    )
-                else:
-                    nc.scalar.activation(out=z[c][:, :, t], in_=h[:, cols], func=ACT.Copy, scale=gn_t[:, t : t + 1])
+                nc.scalar.activation(out=z[c][:, :, t], in_=h[:, cols], func=ACT.Copy, scale=gn_t[:, t : t + 1])
 
         oq = keep.tile([P, S], U32, name="oq", align_bytes=64)
         osc = keep.tile([P, S], U8, name="osc", align_bytes=64)
         out_rows = out_0.rearrange("(p t) c -> p t c", t=PACK)
-        out_words = out_1[0].rearrange("p c r -> p (c r)").bitcast(I32)
-        accs = []
+        banks = []
         for c in range(CHUNKS):
             zq = keep.tile([P, CHUNK], U32, name=f"zq{c}", align_bytes=64)
             zsc = keep.tile([P, CHUNK], U8, name=f"zsc{c}", align_bytes=64)
             nc.vector.quantize_mx(out=zq[:].bitcast(FP8X4), scales=zsc[:], in_=z[c][:].rearrange("p c t -> p (c t)"))
-            acc = psum.tile([P, PACK, CHUNK], F32, name=f"o{c}", tag="bank")
+            parts = PACK if c == CHUNKS - 1 else 1
+            per = PACK // parts
+            accs = [psum.tile([P, PACK, CHUNK], F32, name=f"o{c}_{i}", tag="bank") for i in range(parts)]
             for t in range(PACK):
                 nc.tensor.matmul_mx(
-                    out=acc[:, t, :],
-                    lhsT=w2d[t][:, 0, :].bitcast(FP4X4),
+                    out=accs[t // per][:, t % per, :],
+                    lhsT=w2d[:, t, :].bitcast(FP4X4),
                     lhsT_scale=w2sd[:, t, :],
                     rhs=zq[:].bitcast(FP8X4),
                     rhs_scale=zsc[:],
                     start=True,
                     stop=True,
                 )
-            accs.append(acc)
+            banks.append(accs)
         for c in range(CHUNKS):
             cols = slice(c * CHUNK, (c + 1) * CHUNK)
+            parts = len(banks[c])
+            per = PACK // parts
             o32 = keep.tile([P, PACK, CHUNK], F32, name=f"o32{c}")
-            ob = keep.tile([P, CHUNK, PACK], BF16, name=f"ob{c}", align_bytes=64)
-            if c == CHUNKS - 1:
-                nc.vector.tensor_copy(out=ob[:], in_=accs[c][:].rearrange("p t c -> p c t"))
-            nc.scalar.copy(out=o32[:], in_=accs[c][:])
+            for i in range(parts):
+                if c == 0:
+                    nc.vector.tensor_copy(out=o32[:], in_=banks[c][i][:])
+                else:
+                    nc.scalar.copy(out=o32[:, i * per : (i + 1) * per, :], in_=banks[c][i][:, 0:per, :])
             nc.sync.dma_start(out=out_rows[:, :, cols], in_=o32[:])
-            if c < CHUNKS - 1:
+            parts = min(parts, 2)
+            width = CHUNK // parts
+            obs = [keep.tile([P, width, PACK], BF16, name=f"ob{c}_{i}", align_bytes=64) for i in range(parts)]
+            for i in range(parts):
                 nc.vector.tensor_copy(
-                    out=ob[:].rearrange("p (c i) t -> p c t i", i=4),
-                    in_=o32[:].rearrange("p t (c i) -> p c t i", i=4),
+                    out=obs[i][:].rearrange("p (c i) t -> p c t i", i=4),
+                    in_=o32[:, :, i * width : (i + 1) * width].rearrange("p t (c i) -> p c t i", i=4),
                 )
-            nc.vector.quantize_mx(out=oq[:, cols].bitcast(FP8X4), scales=osc[:, cols], in_=ob[:].rearrange("p c t -> p (c t)"))
-            if c >= CHUNKS - 2:
-                done = slice(0, (c + 1) * CHUNK) if c == CHUNKS - 2 else cols
-                nc.sync.dma_start(out=out_words[:, done], in_=oq[:, done].bitcast(I32))
+            for i in range(parts):
+                part = slice(c * CHUNK + i * width, c * CHUNK + (i + 1) * width)
+                nc.vector.quantize_mx(
+                    out=oq[:, part].bitcast(FP8X4), scales=osc[:, part], in_=obs[i][:].rearrange("p c t -> p (c t)")
+                )
+        nc.sync.dma_start(out=out_1[0].rearrange("p c r -> p (c r)").bitcast(I32), in_=oq[:].bitcast(I32))
         for q in range(4):
-            queue = nc.scalar if q % 2 == 0 else nc.sync
+            queue = nc.sync if q == 3 else nc.scalar
             queue.dma_start(
                 out=out_2[0, 4 * q : 4 * q + 4, :].bitcast(I32),
                 in_=osc[32 * q : 32 * q + 4, :].bitcast(I32),

@@ -96,16 +96,16 @@ def tile_picked_revcoup_none_po_kernel(
         deal_words(nc, w2d, w2w)
         deal_scales(nc, w2sd, w2s)
 
-        z = [keep.tile([P, CHUNK, PACK], BF16, name=f"z{c}", align_bytes=64) for c in range(CHUNKS)]
-        for t in range(PACK):
-            h = keep.tile([P, S], F32, name=f"h{t}")
-            ys = keep.tile([P, S], F32, name=f"ys{t}")
+        zp = [keep.tile([P, PACK, CHUNK], BF16, name=f"zp{c}", align_bytes=64) for c in range(CHUNKS)]
+        def project(t):
             act = keep.tile([P, S], F32, name=f"act{t}")
+            ys = keep.tile([P, S], F32, name=f"ys{t}")
+            parts = []
             for cols in [slice(0, HALF), slice(HALF, S)] if t == 0 else [slice(0, S)]:
-                y = psum.tile([P, S], F32, name=f"y{t}", tag="bank")
-                width = cols.stop - cols.start
+                bank = psum.tile([P, S], F32, name=f"y{t}", tag="bank")
+                y = bank[:, 0 : cols.stop - cols.start]
                 nc.tensor.matmul_mx(
-                    out=y[:, 0:width],
+                    out=y,
                     lhsT=w1d[:, t, :].bitcast(FP4X4),
                     lhsT_scale=w1sd[:, t, :],
                     rhs=xg[:, cols].bitcast(FP8X4),
@@ -113,17 +113,32 @@ def tile_picked_revcoup_none_po_kernel(
                     start=True,
                     stop=True,
                 )
-                nc.scalar.activation(out=act[:, cols], in_=y[:, 0:width], func=ACT.Silu)
-                nc.scalar.copy(out=ys[:, cols], in_=y[:, 0:width])
-            nc.sync.dma_start(out=h[:], in_=ys[:])
+                nc.scalar.activation(out=act[:, cols], in_=y, func=ACT.Silu)
+                nc.scalar.copy(out=ys[:, cols], in_=y)
+                parts.append((cols, y))
             ga = keep.tile([P, V], F32, name=f"ga{t}")
             gb = keep.tile([P, V], F32, name=f"gb{t}")
             nc.vector.tensor_copy(ga[:], act[:].indirect(la_t[:]))
             nc.vector.tensor_copy(gb[:], ys[:].indirect(lb_t[:]))
+            return parts, ga, gb
+
+        def couple(t, parts, ga, gb):
+            h = keep.tile([P, S], F32, name=f"h{t}")
+            for cols, y in parts:
+                nc.scalar.copy(out=h[:, cols], in_=y)
             nc.vector.tensor_tensor(h[:].indirect(lb_t[:]), gb[:], ga[:], ALU.add)
+            return h
+
+        looked_up = [project(0)]
+        hs = []
+        for t in range(PACK):
+            if t + 1 < PACK:
+                looked_up.append(project(t + 1))
+            hs.append(couple(t, *looked_up[t]))
+        for t in range(PACK):
             for c in range(CHUNKS):
                 cols = slice(c * CHUNK, (c + 1) * CHUNK)
-                nc.scalar.activation(out=z[c][:, :, t], in_=h[:, cols], func=ACT.Copy, scale=gn_t[:, t : t + 1])
+                nc.scalar.activation(out=zp[c][:, t, :], in_=hs[t][:, cols], func=ACT.Copy, scale=gn_t[:, t : t + 1])
 
         oq = keep.tile([P, S], U32, name="oq", align_bytes=64)
         osc = keep.tile([P, S], U8, name="osc", align_bytes=64)
@@ -132,7 +147,12 @@ def tile_picked_revcoup_none_po_kernel(
         for c in range(CHUNKS):
             zq = keep.tile([P, CHUNK], U32, name=f"zq{c}", align_bytes=64)
             zsc = keep.tile([P, CHUNK], U8, name=f"zsc{c}", align_bytes=64)
-            nc.vector.quantize_mx(out=zq[:].bitcast(FP8X4), scales=zsc[:], in_=z[c][:].rearrange("p c t -> p (c t)"))
+            z = keep.tile([P, CHUNK, PACK], BF16, name=f"z{c}", align_bytes=64)
+            nc.vector.tensor_copy(
+                out=z[:].rearrange("p (c i) t -> p c t i", i=4),
+                in_=zp[c][:].rearrange("p t (c i) -> p c t i", i=4),
+            )
+            nc.vector.quantize_mx(out=zq[:].bitcast(FP8X4), scales=zsc[:], in_=z[:].rearrange("p c t -> p (c t)"))
             parts = PACK if c == CHUNKS - 1 else 1
             per = PACK // parts
             accs = [psum.tile([P, PACK, CHUNK], F32, name=f"o{c}_{i}", tag="bank") for i in range(parts)]
@@ -153,10 +173,7 @@ def tile_picked_revcoup_none_po_kernel(
             per = PACK // parts
             o32 = keep.tile([P, PACK, CHUNK], F32, name=f"o32{c}")
             for i in range(parts):
-                if c == 0:
-                    nc.vector.tensor_copy(out=o32[:], in_=banks[c][i][:])
-                else:
-                    nc.scalar.copy(out=o32[:, i * per : (i + 1) * per, :], in_=banks[c][i][:, 0:per, :])
+                nc.scalar.copy(out=o32[:, i * per : (i + 1) * per, :], in_=banks[c][i][:, 0:per, :])
             nc.sync.dma_start(out=out_rows[:, :, cols], in_=o32[:])
             parts = min(parts, 2)
             width = CHUNK // parts

@@ -18,13 +18,17 @@ ALU = mybir.AluOpType
 
 P = 128
 PACK = 4
+QUADRANTS = 4
+GROUP = 16
 HALF = S // 2
 CHUNK = 128
 CHUNKS = S // CHUNK
+RUN = 4
+PSUM_BANKS = 8
 
 
 def load_scale_rows(queues, tile, scales):
-    for q in range(4):
+    for q in range(QUADRANTS):
         queues[q].dma_start(
             out=tile[32 * q : 32 * q + 4, :].bitcast(I32),
             in_=scales[0, 4 * q : 4 * q + 4, :].bitcast(I32),
@@ -42,17 +46,40 @@ def deal_scales(nc, dealt, scales):
     nc.vector.tensor_copy(out=dealt[:], in_=scales[:].rearrange("p (m t) -> p t m", t=PACK))
 
 
+def interleave(nc, grouped, slots):
+    nc.vector.tensor_copy(
+        out=grouped.rearrange("p (c i) t -> p c t i", i=RUN),
+        in_=slots.rearrange("p t (c i) -> p c t i", i=RUN),
+    )
+
+
+def quantize(nc, codes, scales, grouped):
+    nc.vector.quantize_mx(out=codes.bitcast(FP8X4), scales=scales, in_=grouped.rearrange("p c t -> p (c t)"))
+
+
+def product(nc, out, weights, weight_scales, codes, scales):
+    nc.tensor.matmul_mx(
+        out=out,
+        lhsT=weights.bitcast(FP4X4),
+        lhsT_scale=weight_scales,
+        rhs=codes.bitcast(FP8X4),
+        rhs_scale=scales,
+        start=True,
+        stop=True,
+    )
+
+
 def tile_picked_revcoup_none_po_kernel(
     tc, x_words, x_scales, w1_words, w1_scales, gn, w2_words, w2_scales, offs, la, lb, out_0, out_1, out_2
 ):
     nc = tc.nc
     with ExitStack() as ctx:
         keep = ctx.enter_context(tc.tile_pool(name="keep", bufs=1))
-        psum = ctx.enter_context(tc.psum_pool(name="psum", bufs=8))
+        psum = ctx.enter_context(tc.psum_pool(name="psum", bufs=PSUM_BANKS))
 
-        offs_t = keep.tile([P, S // 16], U16, name="offs_t")
-        la_t = keep.tile([P, V // 16], U16, name="la_t")
-        lb_t = keep.tile([P, V // 16], U16, name="lb_t")
+        offs_t = keep.tile([P, S // GROUP], U16, name="offs_t")
+        la_t = keep.tile([P, V // GROUP], U16, name="la_t")
+        lb_t = keep.tile([P, V // GROUP], U16, name="lb_t")
         xw = keep.tile([P, T], U32, name="xw", align_bytes=64)
         xs = keep.tile([P, T], U8, name="xs", align_bytes=64)
         w1w = keep.tile([P, 2 * H], U8, name="w1w", align_bytes=64)
@@ -70,61 +97,65 @@ def tile_picked_revcoup_none_po_kernel(
         nc.sync.dma_start(offs_t[:], offs)
         nc.scalar.dma_start(out=w1w[:].bitcast(I32), in_=w1_words[0].bitcast(I32))
         nc.sync.dma_start(la_t[:], la)
-        load_scale_rows([nc.sync, nc.scalar] * 2, xs, x_scales)
+        load_scale_rows([nc.sync, nc.scalar, nc.sync, nc.scalar], xs, x_scales)
         nc.sync.dma_start(out=xw[:].bitcast(I32), in_=x_words[0].rearrange("p c r -> p (c r)").bitcast(I32))
         nc.scalar.activation(out=warm[:, 1:2], in_=warm[:, 0:1], func=ACT.Silu)
-        load_scale_rows([nc.scalar] * 4, w1s, w1_scales)
+        load_scale_rows([nc.scalar] * QUADRANTS, w1s, w1_scales)
         nc.sync.dma_start(lb_t[:], lb)
         nc.sync.dma_start(out=w2w[:].bitcast(I32), in_=w2_words[0].bitcast(I32))
-        load_scale_rows([nc.sync] * 4, w2s, w2_scales)
+        load_scale_rows([nc.sync] * QUADRANTS, w2s, w2_scales)
         nc.sync.dma_start(out=gn_t[:], in_=gn.rearrange("(p t) o -> p (t o)", t=PACK))
 
         xsg = keep.tile([P, S], U8, name="xsg", align_bytes=64)
         w1d = keep.tile([P, PACK, 2 * P], U8, name="w1d", align_bytes=64)
         w1sd = keep.tile([P, PACK, P], U8, name="w1sd", align_bytes=64)
-        w2d = keep.tile([P, PACK, 2 * P], U8, name="w2d", align_bytes=64)
         w2sd = keep.tile([P, PACK, P], U8, name="w2sd", align_bytes=64)
         deal_words(nc, w1d, w1w)
         nc.vector.tensor_copy(xsg[:], xs[:].indirect(offs_t[:]))
+        xg0 = keep.tile([P, HALF], U32, name="xg0", align_bytes=64)
+        nc.vector.tensor_copy(xg0[:], xw[:].indirect(offs_t[:, 0 : HALF // GROUP]))
         deal_scales(nc, w1sd, w1s)
-        xg = keep.tile([P, S], U32, name="xg", tag="w1s", align_bytes=64)
-        for u in range(2):
-            nc.vector.tensor_copy(
-                xg[:, u * HALF : (u + 1) * HALF],
-                xw[:].indirect(offs_t[:, u * HALF // 16 : (u + 1) * HALF // 16]),
-            )
+        xg1 = keep.tile([P, HALF], U32, name="xg1", tag="w1s", align_bytes=64)
+        nc.vector.tensor_copy(xg1[:], xw[:].indirect(offs_t[:, HALF // GROUP : S // GROUP]))
+        xg = [xg0, xg1]
+        w2d = keep.tile([P, PACK, 2 * P], U8, name="w2d", tag="xw", align_bytes=64)
         deal_words(nc, w2d, w2w)
         deal_scales(nc, w2sd, w2s)
 
-        zp = [keep.tile([P, PACK, CHUNK], BF16, name=f"zp{c}", align_bytes=64) for c in range(CHUNKS)]
+        z_pieces = [slice(0, CHUNK // 2), slice(CHUNK // 2, CHUNK)]
+        z_pieces += [slice(c * CHUNK, (c + 1) * CHUNK) for c in range(1, CHUNKS)]
+        z_slots = [
+            keep.tile([P, PACK, piece.stop - piece.start], BF16, name=f"zp{piece.start}", align_bytes=64)
+            for piece in z_pieces
+        ]
+
         def project(t):
             act = keep.tile([P, S], F32, name=f"act{t}")
             ys = keep.tile([P, S], F32, name=f"ys{t}")
-            parts = []
-            for cols in [slice(0, HALF), slice(HALF, S)] if t == 0 else [slice(0, S)]:
+            stretches = []
+            edges = [0, HALF, HALF + CHUNK, S] if t == 0 else [0, S]
+            for lo, hi in zip(edges, edges[1:]):
+                cols = slice(lo, hi)
                 bank = psum.tile([P, S], F32, name=f"y{t}", tag="bank")
-                y = bank[:, 0 : cols.stop - cols.start]
-                nc.tensor.matmul_mx(
-                    out=y,
-                    lhsT=w1d[:, t, :].bitcast(FP4X4),
-                    lhsT_scale=w1sd[:, t, :],
-                    rhs=xg[:, cols].bitcast(FP8X4),
-                    rhs_scale=xsg[:, cols],
-                    start=True,
-                    stop=True,
-                )
+                y = bank[:, 0 : hi - lo]
+                for first in range(lo, hi, HALF):
+                    end = min(first + HALF, hi)
+                    within = first % HALF
+                    codes = xg[first // HALF][:, within : within + end - first]
+                    product(nc, bank[:, first - lo : end - lo], w1d[:, t, :], w1sd[:, t, :], codes, xsg[:, first:end])
                 nc.scalar.activation(out=act[:, cols], in_=y, func=ACT.Silu)
+                stretches.append((cols, y))
+            for cols, y in stretches:
                 nc.scalar.copy(out=ys[:, cols], in_=y)
-                parts.append((cols, y))
             ga = keep.tile([P, V], F32, name=f"ga{t}")
             gb = keep.tile([P, V], F32, name=f"gb{t}")
             nc.vector.tensor_copy(ga[:], act[:].indirect(la_t[:]))
             nc.vector.tensor_copy(gb[:], ys[:].indirect(lb_t[:]))
-            return parts, ga, gb
+            return stretches, ga, gb
 
-        def couple(t, parts, ga, gb):
+        def couple(t, stretches, ga, gb):
             h = keep.tile([P, S], F32, name=f"h{t}")
-            for cols, y in parts:
+            for cols, y in stretches:
                 nc.scalar.copy(out=h[:, cols], in_=y)
             nc.vector.tensor_tensor(h[:].indirect(lb_t[:]), gb[:], ga[:], ALU.add)
             return h
@@ -135,62 +166,56 @@ def tile_picked_revcoup_none_po_kernel(
             if t + 1 < PACK:
                 looked_up.append(project(t + 1))
             hs.append(couple(t, *looked_up[t]))
+
         for t in range(PACK):
-            for c in range(CHUNKS):
-                cols = slice(c * CHUNK, (c + 1) * CHUNK)
-                nc.scalar.activation(out=zp[c][:, t, :], in_=hs[t][:, cols], func=ACT.Copy, scale=gn_t[:, t : t + 1])
+            for slots, piece in zip(z_slots, z_pieces):
+                nc.scalar.activation(out=slots[:, t, :], in_=hs[t][:, piece], func=ACT.Copy, scale=gn_t[:, t : t + 1])
 
         oq = keep.tile([P, S], U32, name="oq", align_bytes=64)
         osc = keep.tile([P, S], U8, name="osc", align_bytes=64)
         out_rows = out_0.rearrange("(p t) c -> p t c", t=PACK)
-        banks = []
+        bank_counts = [2] + [1] * (CHUNKS - 2) + [PACK]
+        out_banks = []
         for c in range(CHUNKS):
             zq = keep.tile([P, CHUNK], U32, name=f"zq{c}", align_bytes=64)
             zsc = keep.tile([P, CHUNK], U8, name=f"zsc{c}", align_bytes=64)
-            z = keep.tile([P, CHUNK, PACK], BF16, name=f"z{c}", align_bytes=64)
-            nc.vector.tensor_copy(
-                out=z[:].rearrange("p (c i) t -> p c t i", i=4),
-                in_=zp[c][:].rearrange("p t (c i) -> p c t i", i=4),
-            )
-            nc.vector.quantize_mx(out=zq[:].bitcast(FP8X4), scales=zsc[:], in_=z[:].rearrange("p c t -> p (c t)"))
-            parts = PACK if c == CHUNKS - 1 else 1
-            per = PACK // parts
-            accs = [psum.tile([P, PACK, CHUNK], F32, name=f"o{c}_{i}", tag="bank") for i in range(parts)]
+            grouped = []
+            for slots, piece in zip(z_slots, z_pieces):
+                if piece.start // CHUNK == c:
+                    z = keep.tile([P, piece.stop - piece.start, PACK], BF16, name=f"z{piece.start}", align_bytes=64)
+                    interleave(nc, z[:], slots[:])
+                    grouped.append((z, slice(piece.start - c * CHUNK, piece.stop - c * CHUNK)))
+            for z, local in grouped:
+                quantize(nc, zq[:, local], zsc[:, local], z[:])
+            per_bank = PACK // bank_counts[c]
+            accs = [psum.tile([P, PACK, CHUNK], F32, name=f"o{c}_{i}", tag="bank") for i in range(bank_counts[c])]
             for t in range(PACK):
-                nc.tensor.matmul_mx(
-                    out=accs[t // per][:, t % per, :],
-                    lhsT=w2d[:, t, :].bitcast(FP4X4),
-                    lhsT_scale=w2sd[:, t, :],
-                    rhs=zq[:].bitcast(FP8X4),
-                    rhs_scale=zsc[:],
-                    start=True,
-                    stop=True,
-                )
-            banks.append(accs)
+                product(nc, accs[t // per_bank][:, t % per_bank, :], w2d[:, t, :], w2sd[:, t, :], zq[:], zsc[:])
+            out_banks.append(accs)
+
         for c in range(CHUNKS):
             cols = slice(c * CHUNK, (c + 1) * CHUNK)
-            parts = len(banks[c])
-            per = PACK // parts
+            per_bank = PACK // bank_counts[c]
             o32 = keep.tile([P, PACK, CHUNK], F32, name=f"o32{c}")
-            for i in range(parts):
-                nc.scalar.copy(out=o32[:, i * per : (i + 1) * per, :], in_=banks[c][i][:, 0:per, :])
-            nc.sync.dma_start(out=out_rows[:, :, cols], in_=o32[:])
-            parts = min(parts, 2)
-            width = CHUNK // parts
-            obs = [keep.tile([P, width, PACK], BF16, name=f"ob{c}_{i}", align_bytes=64) for i in range(parts)]
-            for i in range(parts):
-                nc.vector.tensor_copy(
-                    out=obs[i][:].rearrange("p (c i) t -> p c t i", i=4),
-                    in_=o32[:, :, i * width : (i + 1) * width].rearrange("p t (c i) -> p c t i", i=4),
-                )
-            for i in range(parts):
-                part = slice(c * CHUNK + i * width, c * CHUNK + (i + 1) * width)
-                nc.vector.quantize_mx(
-                    out=oq[:, part].bitcast(FP8X4), scales=osc[:, part], in_=obs[i][:].rearrange("p c t -> p (c t)")
-                )
+            for i, acc in enumerate(out_banks[c]):
+                ts = slice(i * per_bank, (i + 1) * per_bank)
+                nc.scalar.copy(out=o32[:, ts, :], in_=acc[:, 0:per_bank, :])
+                if c == 0:
+                    nc.sync.dma_start(out=out_rows[:, ts, cols], in_=o32[:, ts, :])
+            if c > 0:
+                nc.sync.dma_start(out=out_rows[:, :, cols], in_=o32[:])
+            width = CHUNK // 2 if c == CHUNKS - 1 else CHUNK
+            starts = range(0, CHUNK, width)
+            obs = [keep.tile([P, width, PACK], BF16, name=f"ob{c}_{lo // width}", align_bytes=64) for lo in starts]
+            for ob, lo in zip(obs, starts):
+                interleave(nc, ob[:], o32[:, :, lo : lo + width])
+            for ob, lo in zip(obs, starts):
+                done = slice(c * CHUNK + lo, c * CHUNK + lo + width)
+                quantize(nc, oq[:, done], osc[:, done], ob[:])
+
         nc.sync.dma_start(out=out_1[0].rearrange("p c r -> p (c r)").bitcast(I32), in_=oq[:].bitcast(I32))
-        for q in range(4):
-            queue = nc.sync if q == 3 else nc.scalar
+        for q in range(QUADRANTS):
+            queue = nc.sync if q == QUADRANTS - 1 else nc.scalar
             queue.dma_start(
                 out=out_2[0, 4 * q : 4 * q + 4, :].bitcast(I32),
                 in_=osc[32 * q : 32 * q + 4, :].bitcast(I32),

from contextlib import ExitStack

import concourse.mybir as mybir

K, T, S, V, H, N = 512, 2048, 512, 256, 512, 512
FLOPS = 2 * K * H * S + 2 * H * N * S

F32 = mybir.dt.float32
BF16 = mybir.dt.bfloat16
I32 = mybir.dt.int32
U32 = mybir.dt.uint32
U16 = mybir.dt.uint16
U8 = mybir.dt.uint8
FP8X4 = mybir.dt.float8_e4m3fn_x4
FP4X4 = mybir.dt.float4_e2m1fn_x4
ACT = mybir.ActivationFunctionType
ALU = mybir.AluOpType

P = 128
PACK = 4
QUADRANTS = 4
GROUP = 16
HALF = S // 2
CHUNK = 128
CHUNKS = S // CHUNK
RUN = 4
PSUM_BANKS = 8


def load_scale_rows(queues, tile, scales):
    for q in range(QUADRANTS):
        queues[q].dma_start(
            out=tile[32 * q : 32 * q + 4, :].bitcast(I32),
            in_=scales[0, 4 * q : 4 * q + 4, :].bitcast(I32),
        )


def deal_words(nc, dealt, words):
    nc.vector.tensor_copy(
        out=dealt[:].rearrange("p t (m b) -> p t m b", b=2),
        in_=words[:].rearrange("p (m t b) -> p t m b", t=PACK, b=2),
    )


def deal_scales(nc, dealt, scales):
    nc.vector.tensor_copy(out=dealt[:], in_=scales[:].rearrange("p (m t) -> p t m", t=PACK))


def interleave(nc, grouped, slots):
    nc.vector.tensor_copy(
        out=grouped.rearrange("p (c i) t -> p c t i", i=RUN),
        in_=slots.rearrange("p t (c i) -> p c t i", i=RUN),
    )


def quantize(nc, codes, scales, grouped):
    nc.vector.quantize_mx(out=codes.bitcast(FP8X4), scales=scales, in_=grouped.rearrange("p c t -> p (c t)"))


def product(nc, out, weights, weight_scales, codes, scales):
    nc.tensor.matmul_mx(
        out=out,
        lhsT=weights.bitcast(FP4X4),
        lhsT_scale=weight_scales,
        rhs=codes.bitcast(FP8X4),
        rhs_scale=scales,
        start=True,
        stop=True,
    )


def tile_picked_revcoup_none_po_kernel(
    tc, x_words, x_scales, w1_words, w1_scales, gn, w2_words, w2_scales, offs, la, lb, out_0, out_1, out_2
):
    nc = tc.nc
    with ExitStack() as ctx:
        keep = ctx.enter_context(tc.tile_pool(name="keep", bufs=1))
        psum = ctx.enter_context(tc.psum_pool(name="psum", bufs=PSUM_BANKS))

        offs_t = keep.tile([P, S // GROUP], U16, name="offs_t")
        la_t = keep.tile([P, V // GROUP], U16, name="la_t")
        lb_t = keep.tile([P, V // GROUP], U16, name="lb_t")
        xw = keep.tile([P, T], U32, name="xw", align_bytes=64)
        xs = keep.tile([P, T], U8, name="xs", align_bytes=64)
        w1w = keep.tile([P, 2 * H], U8, name="w1w", align_bytes=64)
        w1s = keep.tile([P, H], U8, name="w1s", align_bytes=64)
        w2w = keep.tile([P, 2 * N], U8, name="w2w", align_bytes=64)
        w2s = keep.tile([P, N], U8, name="w2s", align_bytes=64)
        gn_t = keep.tile([P, PACK], F32, name="gn_t")
        warm = keep.tile([P, 2], F32, name="warm")

        nc.vector.memset(xs[:].bitcast(I32), 0)
        nc.vector.memset(w1s[:].bitcast(I32), 0)
        nc.vector.memset(w2s[:].bitcast(I32), 0)
        nc.vector.memset(warm[:, 0:1], 0.0)

        nc.sync.dma_start(offs_t[:], offs)
        nc.scalar.dma_start(out=w1w[:].bitcast(I32), in_=w1_words[0].bitcast(I32))
        nc.sync.dma_start(la_t[:], la)
        load_scale_rows([nc.sync, nc.scalar, nc.sync, nc.scalar], xs, x_scales)
        nc.sync.dma_start(out=xw[:].bitcast(I32), in_=x_words[0].rearrange("p c r -> p (c r)").bitcast(I32))
        nc.scalar.activation(out=warm[:, 1:2], in_=warm[:, 0:1], func=ACT.Silu)
        load_scale_rows([nc.scalar] * QUADRANTS, w1s, w1_scales)
        nc.sync.dma_start(lb_t[:], lb)
        nc.sync.dma_start(out=w2w[:].bitcast(I32), in_=w2_words[0].bitcast(I32))
        load_scale_rows([nc.sync] * QUADRANTS, w2s, w2_scales)
        nc.sync.dma_start(out=gn_t[:], in_=gn.rearrange("(p t) o -> p (t o)", t=PACK))

        xsg = keep.tile([P, S], U8, name="xsg", align_bytes=64)
        w1d = keep.tile([P, PACK, 2 * P], U8, name="w1d", align_bytes=64)
        w1sd = keep.tile([P, PACK, P], U8, name="w1sd", align_bytes=64)
        w2sd = keep.tile([P, PACK, P], U8, name="w2sd", align_bytes=64)
        deal_words(nc, w1d, w1w)
        nc.vector.tensor_copy(xsg[:], xs[:].indirect(offs_t[:]))
        xg0 = keep.tile([P, HALF], U32, name="xg0", align_bytes=64)
        nc.vector.tensor_copy(xg0[:], xw[:].indirect(offs_t[:, 0 : HALF // GROUP]))
        deal_scales(nc, w1sd, w1s)
        xg1 = keep.tile([P, HALF], U32, name="xg1", tag="w1s", align_bytes=64)
        nc.vector.tensor_copy(xg1[:], xw[:].indirect(offs_t[:, HALF // GROUP : S // GROUP]))
        xg = [xg0, xg1]
        w2d = keep.tile([P, PACK, 2 * P], U8, name="w2d", tag="xw", align_bytes=64)
        deal_words(nc, w2d, w2w)
        deal_scales(nc, w2sd, w2s)

        z_pieces = [slice(0, CHUNK // 2), slice(CHUNK // 2, CHUNK)]
        z_pieces += [slice(c * CHUNK, (c + 1) * CHUNK) for c in range(1, CHUNKS)]
        z_slots = [
            keep.tile([P, PACK, piece.stop - piece.start], BF16, name=f"zp{piece.start}", align_bytes=64)
            for piece in z_pieces
        ]

        def project(t):
            act = keep.tile([P, S], F32, name=f"act{t}")
            ys = keep.tile([P, S], F32, name=f"ys{t}")
            stretches = []
            edges = [0, HALF, HALF + CHUNK, S] if t == 0 else [0, S]
            for lo, hi in zip(edges, edges[1:]):
                cols = slice(lo, hi)
                bank = psum.tile([P, S], F32, name=f"y{t}", tag="bank")
                y = bank[:, 0 : hi - lo]
                for first in range(lo, hi, HALF):
                    end = min(first + HALF, hi)
                    within = first % HALF
                    codes = xg[first // HALF][:, within : within + end - first]
                    product(nc, bank[:, first - lo : end - lo], w1d[:, t, :], w1sd[:, t, :], codes, xsg[:, first:end])
                nc.scalar.activation(out=act[:, cols], in_=y, func=ACT.Silu)
                stretches.append((cols, y))
            for cols, y in stretches:
                nc.scalar.copy(out=ys[:, cols], in_=y)
            ga = keep.tile([P, V], F32, name=f"ga{t}")
            gb = keep.tile([P, V], F32, name=f"gb{t}")
            nc.vector.tensor_copy(ga[:], act[:].indirect(la_t[:]))
            nc.vector.tensor_copy(gb[:], ys[:].indirect(lb_t[:]))
            return stretches, ga, gb

        def couple(t, stretches, ga, gb):
            h = keep.tile([P, S], F32, name=f"h{t}")
            for cols, y in stretches:
                nc.scalar.copy(out=h[:, cols], in_=y)
            nc.vector.tensor_tensor(h[:].indirect(lb_t[:]), gb[:], ga[:], ALU.add)
            return h

        looked_up = [project(0)]
        hs = []
        for t in range(PACK):
            if t + 1 < PACK:
                looked_up.append(project(t + 1))
            hs.append(couple(t, *looked_up[t]))

        for t in range(PACK):
            for slots, piece in zip(z_slots, z_pieces):
                nc.scalar.activation(out=slots[:, t, :], in_=hs[t][:, piece], func=ACT.Copy, scale=gn_t[:, t : t + 1])

        oq = keep.tile([P, S], U32, name="oq", align_bytes=64)
        osc = keep.tile([P, S], U8, name="osc", align_bytes=64)
        out_rows = out_0.rearrange("(p t) c -> p t c", t=PACK)
        bank_counts = [2] + [1] * (CHUNKS - 2) + [PACK]
        out_banks = []
        for c in range(CHUNKS):
            zq = keep.tile([P, CHUNK], U32, name=f"zq{c}", align_bytes=64)
            zsc = keep.tile([P, CHUNK], U8, name=f"zsc{c}", align_bytes=64)
            grouped = []
            for slots, piece in zip(z_slots, z_pieces):
                if piece.start // CHUNK == c:
                    z = keep.tile([P, piece.stop - piece.start, PACK], BF16, name=f"z{piece.start}", align_bytes=64)
                    interleave(nc, z[:], slots[:])
                    grouped.append((z, slice(piece.start - c * CHUNK, piece.stop - c * CHUNK)))
            for z, local in grouped:
                quantize(nc, zq[:, local], zsc[:, local], z[:])
            per_bank = PACK // bank_counts[c]
            accs = [psum.tile([P, PACK, CHUNK], F32, name=f"o{c}_{i}", tag="bank") for i in range(bank_counts[c])]
            for t in range(PACK):
                product(nc, accs[t // per_bank][:, t % per_bank, :], w2d[:, t, :], w2sd[:, t, :], zq[:], zsc[:])
            out_banks.append(accs)

        for c in range(CHUNKS):
            cols = slice(c * CHUNK, (c + 1) * CHUNK)
            per_bank = PACK // bank_counts[c]
            o32 = keep.tile([P, PACK, CHUNK], F32, name=f"o32{c}")
            for i, acc in enumerate(out_banks[c]):
                ts = slice(i * per_bank, (i + 1) * per_bank)
                nc.scalar.copy(out=o32[:, ts, :], in_=acc[:, 0:per_bank, :])
                if c == 0:
                    nc.sync.dma_start(out=out_rows[:, ts, cols], in_=o32[:, ts, :])
            if c > 0:
                nc.sync.dma_start(out=out_rows[:, :, cols], in_=o32[:])
            width = CHUNK // 2 if c == CHUNKS - 1 else CHUNK
            starts = range(0, CHUNK, width)
            obs = [keep.tile([P, width, PACK], BF16, name=f"ob{c}_{lo // width}", align_bytes=64) for lo in starts]
            for ob, lo in zip(obs, starts):
                interleave(nc, ob[:], o32[:, :, lo : lo + width])
            for ob, lo in zip(obs, starts):
                done = slice(c * CHUNK + lo, c * CHUNK + lo + width)
                quantize(nc, oq[:, done], osc[:, done], ob[:])

        nc.sync.dma_start(out=out_1[0].rearrange("p c r -> p (c r)").bitcast(I32), in_=oq[:].bitcast(I32))
        for q in range(QUADRANTS):
            queue = nc.sync if q == QUADRANTS - 1 else nc.scalar
            queue.dma_start(
                out=out_2[0, 4 * q : 4 * q + 4, :].bitcast(I32),
                in_=osc[32 * q : 32 * q + 4, :].bitcast(I32),
            )
